import numpy as np
import ml_dtypes


def mxq(x, axis, fmt="e4m3"):
    dtype, down = {"e4m3": (ml_dtypes.float8_e4m3fn, 7), "e5m2": (ml_dtypes.float8_e5m2, 14)}[fmt]
    v = np.moveaxis(np.asarray(x, np.float32).astype(ml_dtypes.bfloat16).astype(np.float64), axis, -1)
    blocks = v.reshape(v.shape[:-1] + (-1, 32))
    amax = np.abs(blocks).max(-1, keepdims=True)
    byte = np.maximum(np.where(amax > 0, np.frexp(amax)[1] - 1 + 127, 0) - down, 1)
    scale = np.exp2(byte - 127.0)
    codes = (blocks / scale).astype(np.float32).astype(dtype).astype(np.float64)
    return np.moveaxis((codes * scale).reshape(v.shape), -1, axis)


WIDE = False


def mx_kscale(k):
    if not WIDE:
        return np.ones(k)
    levels = np.array([10, -10, 5, -5, 0])
    if k % 512:
        return np.exp2(np.random.permutation(np.resize(levels, k // 32))).repeat(32)
    a = np.empty((k // 512, 16))
    for p in range(k // 512):
        a[p, :8] = np.random.permutation(np.resize(levels, 8))
        for g in range(8):
            far = levels[np.abs(levels - a[p, g]) >= 10]
            a[p, g + 8] = far[np.random.randint(len(far))]
    return np.exp2(a.ravel()).repeat(32)


def f64(x):
    return np.asarray(x).astype(np.float64)


def striped(idx):
    return np.tile(idx.reshape(-1, 16).T, (8, 1)).astype(np.uint16)


def unstriped(offs):
    return offs[:16].T.reshape(-1).astype(np.int64)


def pack_weight(w):
    k, n = w.shape
    w = f64(np.asarray(w, np.float32).astype(ml_dtypes.bfloat16)).reshape(k // 32, 32, n)
    amax = np.abs(w).max(1)
    byte = np.clip(np.where(amax > 0, np.frexp(amax)[1] - 1 + 127 - 7, 1), 1, 254)
    scaled = (w * np.exp2(127.0 - byte)[:, None, :]).reshape(k, n).astype(np.float32)
    words = np.ascontiguousarray(scaled.reshape(k // 512, 128, 4, n).transpose(0, 1, 3, 2)).astype(ml_dtypes.float8_e4m3fn).view(np.uint8)
    return words, np.ascontiguousarray(byte.astype(np.uint8).reshape(k // 512, 16, n))


def unpack_weight(words, scales):
    g, p, n, _ = words.shape
    vals = np.ascontiguousarray(words).view(ml_dtypes.float8_e4m3fn).astype(np.float64) * np.repeat(np.exp2(scales.astype(np.float64) - 127.0), 8, axis=1)[..., None]
    return vals.transpose(0, 1, 3, 2).reshape(g * 512, n)


E2M1 = np.array([0.0, 0.5, 1.0, 1.5, 2.0, 3.0, 4.0, 6.0, -0.0, -0.5, -1.0, -1.5, -2.0, -3.0, -4.0, -6.0])


def pack_fp4(w):
    k, n = w.shape
    w = f64(np.asarray(w, np.float32).astype(ml_dtypes.bfloat16)).reshape(k // 32, 32, n)
    amax = np.abs(w).max(1)
    mant, ex = np.frexp(amax / 6.0)
    byte = np.clip(np.where(amax > 0, np.where(mant > 0.5, ex, ex - 1) + 127, 1), 1, 254)
    scaled = (w * np.exp2(127.0 - byte)[:, None, :]).reshape(k, n).astype(np.float32)
    c = np.ascontiguousarray(scaled.reshape(k // 512, 128, 4, n).transpose(0, 1, 3, 2)).astype(ml_dtypes.float4_e2m1fn).view(np.uint8) & 0xF
    words = (c[..., 0::2] | (c[..., 1::2] << 4)).reshape(k // 512, 128, 2 * n)
    return np.ascontiguousarray(words), np.ascontiguousarray(byte.astype(np.uint8).reshape(k // 512, 16, n))


def unpack_fp4(words, scales):
    g, _, n = scales.shape
    words = np.ascontiguousarray(words).reshape(g, 128, n, 2)
    nib = np.empty((g, 128, n, 4), np.uint8)
    nib[..., 0::2] = words & 0xF
    nib[..., 1::2] = words >> 4
    vals = E2M1[nib] * np.repeat(np.exp2(scales.astype(np.float64) - 127.0), 8, axis=1)[..., None]
    return vals.transpose(0, 1, 3, 2).reshape(g * 512, n)


def sigmoid(v):
    return 1.0 / (1.0 + np.exp(-np.maximum(v, -700.0)))

def planes(y):
    n, m = y.shape
    v = y.astype(np.float32).astype(ml_dtypes.bfloat16).astype(np.float64).reshape(n // 32, 32, m)
    top = np.abs(v).max(1)
    byte = np.clip(np.where(top > 0, np.frexp(top)[1] - 1 + 127 - 7, 1), 1, 254)
    codes = (v * np.exp2(127.0 - byte)[:, None, :]).reshape(n, m).astype(np.float32).astype(ml_dtypes.float8_e4m3fn).view(np.uint8)
    words = codes.reshape(n // 512, 128, 4, m).transpose(0, 1, 3, 2)
    return np.ascontiguousarray(words), np.ascontiguousarray(byte.astype(np.uint8).reshape(n // 512, 16, m))


K, T, S, N, H, W, C = 512, 2048, 512, 512, 512, 2048, 512


def setup_inputs():
    n = np.random.standard_normal
    s = mx_kscale(K)[:, None]
    u = mx_kscale(S)
    packed_xT = pack_weight(n((K, T)) * s)
    packed_w1 = pack_fp4(n((K, H)) / np.sqrt(K) / s)
    packed_w2 = pack_fp4(n((H, N)) / np.sqrt(H) / u[:, None])
    return {
        "x_words": packed_xT[0],
        "x_scales": packed_xT[1],
        "w1_words": packed_w1[0],
        "w1_scales": packed_w1[1],
        "gn": (np.random.uniform(0.5, 1.5, (H, 1)) * u[:, None]).astype(np.float32),
        "w2_words": packed_w2[0],
        "w2_scales": packed_w2[1],
        "gs": (np.random.uniform(0.5, 1.5, (K, 1)) / s).astype(np.float32),
        "offs": striped(np.random.permutation(T)[:S]),
        "n1": striped(np.random.randint(0, S, W)),
        "n2": striped(np.random.permutation(S)),
        "cand": striped(np.random.permutation(T)[:C]),
        "n3": striped(np.random.permutation(S)),
        "n4": striped(np.random.permutation(S)),
    }


def reference(x_words, x_scales, w1_words, w1_scales, gn, w2_words, w2_scales, gs, offs, n1, n2, cand, n3, n4):
    xq = unpack_weight(x_words, x_scales)[:, unstriped(offs)]
    y = unpack_fp4(w1_words, w1_scales).T @ xq
    mb = y[:, unstriped(n1)]
    sq = (mb) ** 2
    qs = sq.reshape(H, S, 4).sum(axis=2)
    z = f64(gn) * (y / np.sqrt(qs + 0.5))
    a = unpack_fp4(w2_words, w2_scales).T @ mxq(z, 0, "e4m3")
    x_cand = unpack_weight(x_words, x_scales)[:, unstriped(cand)]
    z2 = f64(gs) * (np.maximum(y, y[:, unstriped(n2)]))
    b = 0.0625 * ((x_cand.T @ mxq(z2, 0, "e4m3")))
    out_0 = a + (sigmoid(b[:, unstriped(n4)] - b)) * (a[:, unstriped(n3)] - a)
    return (out_0,) + planes(out_0)

@@ -1,0 +1,257 @@
+from contextlib import ExitStack
+
+import concourse.mybir as mybir
+from concourse.masks import make_identity
+
+K, T, S, W = 512, 2048, 512, 2048
+FLOPS = 3 * 2 * 512 * 512 * 512
+
+F32 = mybir.dt.float32
+BF16 = mybir.dt.bfloat16
+I32 = mybir.dt.int32
+U32 = mybir.dt.uint32
+U16 = mybir.dt.uint16
+U8 = mybir.dt.uint8
+FP8X4 = mybir.dt.float8_e4m3fn_x4
+FP4X4 = mybir.dt.float4_e2m1fn_x4
+ACT = mybir.ActivationFunctionType
+ALU = mybir.AluOpType
+
+P = 128
+PACK = 4
+MEMBERS = 4
+HALF = 256
+BLOCKS = S // P
+
+
+def tile_picked_fkcdpullbgvarbig_none_po_kernel(
+    tc, x_words, x_scales, w1_words, w1_scales, gn, w2_words, w2_scales, gs, offs, n1, n2, cand, n3, n4, out_0, out_1, out_2
+):
+    nc = tc.nc
+    with ExitStack() as ctx:
+        keep = ctx.enter_context(tc.tile_pool(name="keep", bufs=1))
+        ring = ctx.enter_context(tc.tile_pool(name="ring", bufs=1))
+        psum = ctx.enter_context(tc.psum_pool(name="psum", bufs=1))
+
+        def held(name, shape, dtype):
+            return keep.tile(shape, dtype, name=name, align_bytes=64)
+
+        def load_list(name, src):
+            tile = keep.tile(list(src.shape), U16, name=name)
+            nc.sync.dma_start(tile[:], src)
+            return tile
+
+        def load_scale_quadrants(queue, name, src):
+            width = src.shape[2]
+            plane = held(name, [P, width], U8)
+            for q in range(4):
+                rows = src[0, 4 * q : 4 * q + 4, :].bitcast(I32)
+                queue.dma_start(plane[32 * q : 32 * (q + 1), :].bitcast(I32), rows.unsqueeze(0).to_broadcast([8, 4, width // 4]))
+            return plane
+
+        def deal_weight(name, words, scales):
+            dealt_words = held(name + "_words", [P, 2 * S], U8)
+            nc.scalar.copy(
+                dealt_words[:].bitcast(U16).rearrange("p (t m) -> p t m", t=PACK),
+                words[:].bitcast(U16).rearrange("p (m t) -> p t m", t=PACK),
+            )
+            dealt_scales = held(name + "_scales", [P, S], U8)
+            nc.vector.tensor_copy(
+                dealt_scales[:].rearrange("p (t m) -> p m t", t=PACK),
+                scales[:].rearrange("p (m t) -> p m t", t=PACK),
+            )
+            return dealt_words, dealt_scales
+
+        def entries(tile, start, count):
+            return tile[:, start // 16 : (start + count) // 16]
+
+        def gather(engine, out, window, offsets):
+            if engine == "vector":
+                nc.vector.tensor_copy(out, window.indirect(offsets))
+            else:
+                nc.scalar.activation(out, window.indirect(offsets), ACT.Copy)
+
+        offs_sb = load_list("offs_sb", offs)
+        cand_sb = load_list("cand_sb", cand)
+        xs = load_scale_quadrants(nc.sync, "xs", x_scales)
+        w1w_raw = held("w1w_raw", [P, 2 * S], U8)
+        nc.sync.dma_start(w1w_raw[:].bitcast(I32), w1_words[0].bitcast(I32))
+        xw = held("xw", [P, T], I32)
+        nc.sync.dma_start(xw[:], x_words[0].rearrange("p c r -> p (c r)").bitcast(I32))
+        w1s_raw = load_scale_quadrants(nc.sync, "w1s_raw", w1_scales)
+        n1_sb = load_list("n1_sb", n1)
+        n2_sb = load_list("n2_sb", n2)
+        n4_sb = load_list("n4_sb", n4)
+        n3_sb = load_list("n3_sb", n3)
+        ident = held("ident", [P, P], F32)
+        make_identity(nc, ident[:])
+        gn_sb = held("gn_sb", [P, PACK], F32)
+        nc.gpsimd.dma_start(gn_sb[:], gn.rearrange("(p t) o -> p (t o)", t=PACK))
+        gs_sb = held("gs_sb", [P, PACK], F32)
+        nc.gpsimd.dma_start(gs_sb[:], gs.rearrange("(p t) o -> p (t o)", t=PACK))
+        w2w_raw = held("w2w_raw", [P, 2 * S], U8)
+        nc.sync.dma_start(w2w_raw[:].bitcast(I32), w2_words[0].bitcast(I32))
+        w2s_raw = load_scale_quadrants(nc.sync, "w2s_raw", w2_scales)
+
+        xq_scales = held("xq_scales", [P, S], U8)
+        nc.vector.tensor_copy(xq_scales[:], xs[:].indirect(offs_sb[:]))
+        xc_scales = held("xc_scales", [P, S], U8)
+        nc.vector.tensor_copy(xc_scales[:].rearrange("p (t m) -> p m t", t=PACK), xs[:].indirect(cand_sb[:]))
+        xq_words = held("xq_words", [P, S], U32)
+        nc.vector.tensor_copy(xq_words[:], xw[:].bitcast(U32).indirect(offs_sb[:]))
+
+        w1w, w1s = deal_weight("w1", w1w_raw, w1s_raw)
+
+        def weight_product(tag, words, scales, codes, code_scales, t):
+            bank = psum.tile([P, S], F32, name=tag, tag=tag)
+            nc.tensor.matmul_mx(
+                out=bank[:],
+                lhsT=words[:, 2 * P * t : 2 * P * (t + 1)].bitcast(FP4X4),
+                lhsT_scale=scales[:, P * t : P * (t + 1)],
+                rhs=codes[:].bitcast(FP8X4),
+                rhs_scale=code_scales[:],
+                start=True,
+                stop=True,
+            )
+            return bank
+
+        y_ps, ysq = [], []
+        for t in range(PACK):
+            y_ps.append(weight_product("bank%d" % t, w1w, w1s, xq_words, xq_scales, t))
+            ysq.append(held("ysq%d" % t, [P, S], F32))
+            nc.scalar.activation(ysq[t][:], y_ps[t][:], ACT.Square)
+
+        xc_words = held("xc_words", [P, S], U32)
+        nc.vector.tensor_copy(xc_words[:].rearrange("p (t m) -> p m t", t=PACK), xw[:].bitcast(U32).indirect(cand_sb[:]))
+
+        y = [held("y%d" % t, [P, S], F32) for t in range(PACK)]
+        yg = held("yg", [P, PACK, S], F32)
+        root_then_gate = held("root_then_gate", [P, PACK, S], F32)
+        z_codes = held("z_codes", [P, S], U32)
+        z_scales = held("z_scales", [P, S], U8)
+        larger = held("larger", [P, PACK, S], F32)
+
+        def member_sums(jb):
+            sums = psum.tile([P, PACK, P], F32, name="sums", tag="bank%d" % (4 + jb % 2))
+            for t in (0, 2, 1, 3):
+                fetched = ring.tile([P, MEMBERS * P], F32, name="fetched", tag="fetched", bufs=8)
+                on_vector = t < 2
+                for h in range(2):
+                    offsets = entries(n1_sb, MEMBERS * P * jb + HALF * h, HALF)
+                    if on_vector:
+                        planes = fetched[:].rearrange("p (m j) -> p j m", m=MEMBERS)
+                        gather("vector", planes[:, 64 * h : 64 * (h + 1), :], ysq[t][:], offsets)
+                    else:
+                        gather("scalar", fetched[:, HALF * h : HALF * (h + 1)], ysq[t][:], offsets)
+                for m in range(MEMBERS):
+                    member = fetched[:, P * m : P * (m + 1)] if on_vector else fetched[:, m : MEMBERS * P : MEMBERS]
+                    nc.tensor.matmul(sums[:, t, :], member, ident[:], start=(m == 0), stop=(m == MEMBERS - 1), is_transpose=True)
+            return sums
+
+        def finish_z(jb, sums):
+            cols = slice(P * jb, P * (jb + 1))
+            nc.scalar.activation(root_then_gate[:, :, cols], sums[:], ACT.Abs_reciprocal_sqrt, bias=0.5)
+            back = psum.tile([P, PACK, P], F32, name="back", tag="bank%d" % (6 + jb % 2))
+            for t in range(PACK):
+                nc.tensor.transpose(back[:, t, :], root_then_gate[:, t, cols], ident[:])
+            z = ring.tile([P, PACK * P], BF16, name="z", tag="z", bufs=2, align_bytes=64)
+            nc.vector.tensor_tensor(
+                z[:].rearrange("p (c i t) -> p c t i", i=4, t=PACK),
+                back[:].rearrange("p t (c i) -> p c t i", i=4),
+                yg[:, :, cols].rearrange("p t (c i) -> p c t i", i=4),
+                ALU.mult,
+            )
+            nc.vector.quantize_mx(out=z_codes[:, cols].bitcast(FP8X4), scales=z_scales[:, cols], in_=z[:])
+
+        def larger_of_pair(t):
+            other = ring.tile([P, S], F32, name="other", tag="other", bufs=4)
+            for h in range(2):
+                gather("scalar", other[:, HALF * h : HALF * (h + 1)], y[t][:], entries(n2_sb, HALF * h, HALF))
+            nc.vector.tensor_tensor(larger[:, t, :], other[:], y_ps[t][:], ALU.max)
+
+        sums0 = member_sums(0)
+        for t in range(PACK):
+            if t < 2:
+                nc.vector.tensor_copy(y[t][:], y_ps[t][:])
+            else:
+                nc.scalar.copy(y[t][:], y_ps[t][:])
+            nc.vector.tensor_scalar(yg[:, t, :], y[t][:], gn_sb[:, t : t + 1], None, ALU.mult)
+        sums1 = member_sums(1)
+        finish_z(0, sums0)
+        larger_of_pair(0)
+        larger_of_pair(1)
+        sums2 = member_sums(2)
+        finish_z(1, sums1)
+        larger_of_pair(2)
+        larger_of_pair(3)
+
+        z2 = held("z2", [P, PACK * S], BF16)
+        nc.vector.tensor_tensor(
+            z2[:].rearrange("p (c i t) -> p c t i", i=4, t=PACK),
+            larger[:].rearrange("p t (c i) -> p c t i", i=4),
+            gs_sb[:].unsqueeze(1).unsqueeze(3).to_broadcast([P, S // 4, PACK, 4]),
+            ALU.mult,
+        )
+        z2_codes = held("z2_codes", [P, S], U32)
+        z2_scales = held("z2_scales", [P, S], U8)
+        nc.vector.quantize_mx(out=z2_codes[:].bitcast(FP8X4), scales=z2_scales[:], in_=z2[:])
+        b_ps = []
+        for t in range(PACK):
+            bank = psum.tile([P, S], F32, name="b_ps", tag="bank%d" % t)
+            nc.tensor.matmul_mx(
+                out=bank[:],
+                lhsT=xc_words[:, P * t : P * (t + 1)].bitcast(FP8X4),
+                lhsT_scale=xc_scales[:, P * t : P * (t + 1)],
+                rhs=z2_codes[:].bitcast(FP8X4),
+                rhs_scale=z2_scales[:],
+                start=True,
+                stop=True,
+            )
+            b_ps.append(bank)
+        b = [held("b%d" % t, [P, S], F32) for t in range(PACK)]
+
+        sums3 = member_sums(3)
+        finish_z(2, sums2)
+        for t in (2, 3, 0, 1):
+            nc.scalar.copy(b[t][:], b_ps[t][:])
+        w2w, w2s = deal_weight("w2", w2w_raw, w2s_raw)
+        finish_z(3, sums3)
+        a_ps = {t: weight_product("bank%d" % (4 + (t + 2) % 4), w2w, w2s, z_codes, z_scales, t) for t in (2, 3, 0, 1)}
+
+        a = [held("a%d" % t, [P, S], F32) for t in range(PACK)]
+        gap = [held("gap%d" % t, [P, S], F32) for t in range(PACK)]
+        for t in (2, 0, 3, 1):
+            other = ring.tile([P, S], F32, name="other", tag="other", bufs=4)
+            for h in range(2):
+                gather("vector" if t >= 2 else "scalar", other[:, HALF * h : HALF * (h + 1)], b[t][:], entries(n4_sb, HALF * h, HALF))
+            nc.vector.tensor_tensor(gap[t][:], other[:], b_ps[t][:], ALU.subtract)
+
+        result = held("result", [P, PACK, S], F32)
+        out_codes = held("out_codes", [P, S], U32)
+        out_scales = held("out_scales", [P, S], U8)
+        out_rows = out_0.rearrange("(p t) c -> p t c", t=PACK)
+        out_words = out_1[0].rearrange("p c r -> p (c r)").bitcast(I32)
+        for h in range(2):
+            cols = slice(HALF * h, HALF * (h + 1))
+            for t in (2, 3, 0, 1):
+                if h == 0:
+                    nc.scalar.activation(root_then_gate[:, t, :], gap[t][:], ACT.Sigmoid, scale=0.0625)
+                    nc.scalar.copy(a[t][:], a_ps[t][:])
+                other = ring.tile([P, HALF], F32, name="far", tag="far", bufs=8)
+                gather("scalar", other[:], a[t][:], entries(n3_sb, HALF * h, HALF))
+                step = ring.tile([P, HALF], F32, name="step", tag="step", bufs=2)
+                nc.vector.tensor_tensor(step[:], other[:], a_ps[t][:, cols], ALU.subtract)
+                pull = ring.tile([P, HALF], F32, name="pull", tag="pull", bufs=2)
+                nc.vector.tensor_tensor(pull[:], step[:], root_then_gate[:, t, cols], ALU.mult)
+                nc.vector.tensor_tensor(result[:, t, cols], pull[:], a_ps[t][:, cols], ALU.add)
+            nc.sync.dma_start(out_rows[:, :, cols], result[:, :, cols])
+            rounded = ring.tile([P, PACK * HALF], BF16, name="rounded", tag="rounded", bufs=2, align_bytes=64)
+            nc.vector.tensor_copy(
+                rounded[:].rearrange("p (c i t) -> p c t i", i=4, t=PACK),
+                result[:, :, cols].rearrange("p t (c i) -> p c t i", i=4),
+            )
+            nc.vector.quantize_mx(out=out_codes[:, cols].bitcast(FP8X4), scales=out_scales[:, cols], in_=rounded[:])
+            nc.sync.dma_start(out_words[:, cols], out_codes[:, cols].bitcast(I32))
+        for q in range(4):
+            queue = nc.scalar if q % 2 else nc.sync
+            queue.dma_start(out_2[0, 4 * q : 4 * q + 4, :].bitcast(I32), out_scales[32 * q : 32 * q + 4, :].bitcast(I32))

@@ -20,8 +20,16 @@ ALU = mybir.AluOpType
 P = 128
 PACK = 4
 MEMBERS = 4
-HALF = 256
 BLOCKS = S // P
+N1_VECTOR = [(jb, t) for jb in range(4) for t in (0, 1, 2) if (jb, t) != (2, 2)]
+N2_VECTOR = ()
+N4_VECTOR = (0, 1, 2)
+Y_VECTOR = ()
+B_VECTOR = ()
+A_VECTOR = (0,)
+N3_VECTOR = ((0, 0), (0, 2))
+CHUNKS = ((0, 256), (256, 256))
+TAIL_ORDER = (0, 1, 2, 3)
 
 
 def tile_picked_fkcdpullbgvarbig_none_po_kernel(
@@ -33,8 +41,14 @@ def tile_picked_fkcdpullbgvarbig_none_po_kernel(
         ring = ctx.enter_context(tc.tile_pool(name="ring", bufs=1))
         psum = ctx.enter_context(tc.psum_pool(name="psum", bufs=1))
 
-        def held(name, shape, dtype):
-            return keep.tile(shape, dtype, name=name, align_bytes=64)
+        def held(name, shape, dtype, tag=""):
+            return keep.tile(shape, dtype, name=name, tag=tag or name, align_bytes=64)
+
+        def window(name, width):
+            tile = held(name, [P, width], F32)
+            if width > S:
+                nc.gpsimd.memset(tile[:, S:], 0.0)
+            return tile
 
         def load_list(name, src):
             tile = keep.tile(list(src.shape), U16, name=name)
@@ -49,14 +63,14 @@ def tile_picked_fkcdpullbgvarbig_none_po_kernel(
                 queue.dma_start(plane[32 * q : 32 * (q + 1), :].bitcast(I32), rows.unsqueeze(0).to_broadcast([8, 4, width // 4]))
             return plane
 
-        def deal_weight(name, words, scales):
+        def deal_weight(name, words, scales, byte_engine):
             dealt_words = held(name + "_words", [P, 2 * S], U8)
             nc.scalar.copy(
                 dealt_words[:].bitcast(U16).rearrange("p (t m) -> p t m", t=PACK),
                 words[:].bitcast(U16).rearrange("p (m t) -> p t m", t=PACK),
             )
             dealt_scales = held(name + "_scales", [P, S], U8)
-            nc.vector.tensor_copy(
+            byte_engine.tensor_copy(
                 dealt_scales[:].rearrange("p (t m) -> p m t", t=PACK),
                 scales[:].rearrange("p (m t) -> p m t", t=PACK),
             )
@@ -65,11 +79,17 @@ def tile_picked_fkcdpullbgvarbig_none_po_kernel(
         def entries(tile, start, count):
             return tile[:, start // 16 : (start + count) // 16]
 
-        def gather(engine, out, window, offsets):
-            if engine == "vector":
-                nc.vector.tensor_copy(out, window.indirect(offsets))
+        def gather(on_vector, out, source, offsets):
+            if on_vector:
+                nc.vector.tensor_copy(out, source.indirect(offsets))
             else:
-                nc.scalar.activation(out, window.indirect(offsets), ACT.Copy)
+                nc.scalar.activation(out, source.indirect(offsets), ACT.Copy)
+
+        def leave_psum(on_vector, out, bank):
+            if on_vector:
+                nc.vector.tensor_copy(out, bank)
+            else:
+                nc.scalar.copy(out, bank)
 
         offs_sb = load_list("offs_sb", offs)
         cand_sb = load_list("cand_sb", cand)
@@ -85,10 +105,14 @@ def tile_picked_fkcdpullbgvarbig_none_po_kernel(
         n3_sb = load_list("n3_sb", n3)
         ident = held("ident", [P, P], F32)
         make_identity(nc, ident[:])
+        ysq = [window("ysq%d" % t, 1024 if any((jb, t) in N1_VECTOR for jb in range(BLOCKS)) else 544) for t in range(PACK)]
         gn_sb = held("gn_sb", [P, PACK], F32)
         nc.gpsimd.dma_start(gn_sb[:], gn.rearrange("(p t) o -> p (t o)", t=PACK))
         gs_sb = held("gs_sb", [P, PACK], F32)
         nc.gpsimd.dma_start(gs_sb[:], gs.rearrange("(p t) o -> p (t o)", t=PACK))
+        y = [window("y%d" % t, 704 if t in N2_VECTOR else 544) for t in range(PACK)]
+        b = [window("b%d" % t, 704 if t in N4_VECTOR else 544) for t in range(PACK)]
+        a = [held("a%d" % t, [P, S], F32) for t in range(PACK)]
         w2w_raw = held("w2w_raw", [P, 2 * S], U8)
         nc.sync.dma_start(w2w_raw[:].bitcast(I32), w2_words[0].bitcast(I32))
         w2s_raw = load_scale_quadrants(nc.sync, "w2s_raw", w2_scales)
@@ -99,62 +123,75 @@ def tile_picked_fkcdpullbgvarbig_none_po_kernel(
         nc.vector.tensor_copy(xc_scales[:].rearrange("p (t m) -> p m t", t=PACK), xs[:].indirect(cand_sb[:]))
         xq_words = held("xq_words", [P, S], U32)
         nc.vector.tensor_copy(xq_words[:], xw[:].bitcast(U32).indirect(offs_sb[:]))
+        w1w, w1s = deal_weight("w1", w1w_raw, w1s_raw, nc.vector)
 
-        w1w, w1s = deal_weight("w1", w1w_raw, w1s_raw)
-
-        def weight_product(tag, words, scales, codes, code_scales, t):
-            bank = psum.tile([P, S], F32, name=tag, tag=tag)
+        def weight_product(tag, words, scales, codes, code_scales, t, cols=slice(0, S), bank=None):
+            if bank is None:
+                bank = psum.tile([P, S], F32, name=tag, tag=tag)
             nc.tensor.matmul_mx(
-                out=bank[:],
+                out=bank[:, cols],
                 lhsT=words[:, 2 * P * t : 2 * P * (t + 1)].bitcast(FP4X4),
                 lhsT_scale=scales[:, P * t : P * (t + 1)],
-                rhs=codes[:].bitcast(FP8X4),
-                rhs_scale=code_scales[:],
+                rhs=codes[:, cols].bitcast(FP8X4),
+                rhs_scale=code_scales[:, cols],
                 start=True,
                 stop=True,
             )
             return bank
 
-        y_ps, ysq = [], []
+        y_ps = []
         for t in range(PACK):
             y_ps.append(weight_product("bank%d" % t, w1w, w1s, xq_words, xq_scales, t))
-            ysq.append(held("ysq%d" % t, [P, S], F32))
-            nc.scalar.activation(ysq[t][:], y_ps[t][:], ACT.Square)
+            nc.scalar.activation(ysq[t][:, :S], y_ps[t][:], ACT.Square)
 
-        xc_words = held("xc_words", [P, S], U32)
+        xc_words = held("xc_words", [P, S], U32, tag="w1s_raw")
+        xc_next = lambda: held("after_cand", [P, S], F32, tag="w1s_raw")[:]
         nc.vector.tensor_copy(xc_words[:].rearrange("p (t m) -> p m t", t=PACK), xw[:].bitcast(U32).indirect(cand_sb[:]))
 
-        y = [held("y%d" % t, [P, S], F32) for t in range(PACK)]
         yg = held("yg", [P, PACK, S], F32)
         root_then_gate = held("root_then_gate", [P, PACK, S], F32)
         z_codes = held("z_codes", [P, S], U32)
         z_scales = held("z_scales", [P, S], U8)
-        larger = held("larger", [P, PACK, S], F32)
+        larger = ring.tile([P, PACK, S], F32, name="larger", tag="larger", bufs=1, align_bytes=64)
+        weighted = ring.tile([P, PACK, S], BF16, name="weighted", tag="weighted", bufs=1, align_bytes=64)
+        piece = 512
 
-        def member_sums(jb):
-            sums = psum.tile([P, PACK, P], F32, name="sums", tag="bank%d" % (4 + jb % 2))
-            for t in (0, 2, 1, 3):
-                fetched = ring.tile([P, MEMBERS * P], F32, name="fetched", tag="fetched", bufs=8)
-                on_vector = t < 2
-                for h in range(2):
-                    offsets = entries(n1_sb, MEMBERS * P * jb + HALF * h, HALF)
+        sums = {}
+
+        def slot(tag, count=1):
+            tile = ring.tile([P, count, S], F32, name=tag, tag=tag, bufs=1, align_bytes=64)
+            return [tile[:, k, :] for k in range(count)]
+
+        def member_sums(jb, t, fetched):
+            if jb not in sums:
+                sums[jb] = psum.tile([P, PACK, P], F32, name="sums", tag="bank%d" % (4 + jb))
+            if True:
+                on_vector = (jb, t) in N1_VECTOR
+                for e in range(0, MEMBERS * P, piece):
+                    offsets = entries(n1_sb, MEMBERS * P * jb + e, piece)
                     if on_vector:
-                        planes = fetched[:].rearrange("p (m j) -> p j m", m=MEMBERS)
-                        gather("vector", planes[:, 64 * h : 64 * (h + 1), :], ysq[t][:], offsets)
+                        planes = fetched.rearrange("p (m j) -> p j m", m=MEMBERS)
+                        gather(True, planes[:, e // MEMBERS : (e + piece) // MEMBERS, :], ysq[t][:], offsets)
                     else:
-                        gather("scalar", fetched[:, HALF * h : HALF * (h + 1)], ysq[t][:], offsets)
+                        gather(False, fetched[:, e : e + piece], ysq[t][:], offsets)
                 for m in range(MEMBERS):
                     member = fetched[:, P * m : P * (m + 1)] if on_vector else fetched[:, m : MEMBERS * P : MEMBERS]
-                    nc.tensor.matmul(sums[:, t, :], member, ident[:], start=(m == 0), stop=(m == MEMBERS - 1), is_transpose=True)
-            return sums
+                    nc.tensor.matmul(sums[jb][:, t, :], member, ident[:], start=(m == 0), stop=(m == MEMBERS - 1), is_transpose=True)
 
-        def finish_z(jb, sums):
+        backs = {}
+
+        def roots(jb):
             cols = slice(P * jb, P * (jb + 1))
-            nc.scalar.activation(root_then_gate[:, :, cols], sums[:], ACT.Abs_reciprocal_sqrt, bias=0.5)
-            back = psum.tile([P, PACK, P], F32, name="back", tag="bank%d" % (6 + jb % 2))
+            nc.scalar.activation(root_then_gate[:, :, cols], sums[jb][:], ACT.Abs_reciprocal_sqrt, bias=0.5)
+            back = psum.tile([P, PACK, P], F32, name="back", tag="bank%d" % (4 + jb))
             for t in range(PACK):
                 nc.tensor.transpose(back[:, t, :], root_then_gate[:, t, cols], ident[:])
-            z = ring.tile([P, PACK * P], BF16, name="z", tag="z", bufs=2, align_bytes=64)
+            backs[jb] = back
+
+        def finish_z(jb, tag):
+            cols = slice(P * jb, P * (jb + 1))
+            back = backs[jb]
+            z = ring.tile([P, PACK * P], BF16, name="z", tag=tag, bufs=1, align_bytes=64)
             nc.vector.tensor_tensor(
                 z[:].rearrange("p (c i t) -> p c t i", i=4, t=PACK),
                 back[:].rearrange("p t (c i) -> p c t i", i=4),
@@ -163,90 +200,132 @@ def tile_picked_fkcdpullbgvarbig_none_po_kernel(
             )
             nc.vector.quantize_mx(out=z_codes[:, cols].bitcast(FP8X4), scales=z_scales[:, cols], in_=z[:])
 
+        def fetch_row(on_vector, source, offsets_tile, other):
+            for e in range(0, S, piece):
+                gather(on_vector, other[:, e : e + piece], source[:], entries(offsets_tile, e, piece))
+            return other
+
         def larger_of_pair(t):
-            other = ring.tile([P, S], F32, name="other", tag="other", bufs=4)
-            for h in range(2):
-                gather("scalar", other[:, HALF * h : HALF * (h + 1)], y[t][:], entries(n2_sb, HALF * h, HALF))
+            other = fetch_row(t in N2_VECTOR, y[t], n2_sb, slot("pair%d" % t)[0])
             nc.vector.tensor_tensor(larger[:, t, :], other[:], y_ps[t][:], ALU.max)
+            nc.gpsimd.tensor_scalar(weighted[:, t, :], larger[:, t, :], gs_sb[:, t : t + 1], 0.0, ALU.mult, ALU.add)
 
-        sums0 = member_sums(0)
-        for t in range(PACK):
-            if t < 2:
-                nc.vector.tensor_copy(y[t][:], y_ps[t][:])
-            else:
-                nc.scalar.copy(y[t][:], y_ps[t][:])
-            nc.vector.tensor_scalar(yg[:, t, :], y[t][:], gn_sb[:, t : t + 1], None, ALU.mult)
-        sums1 = member_sums(1)
-        finish_z(0, sums0)
-        larger_of_pair(0)
-        larger_of_pair(1)
-        sums2 = member_sums(2)
-        finish_z(1, sums1)
-        larger_of_pair(2)
-        larger_of_pair(3)
+        def scale_y(t):
+            leave_psum(t in Y_VECTOR, y[t][:, :S], y_ps[t][:])
 
-        z2 = held("z2", [P, PACK * S], BF16)
-        nc.vector.tensor_tensor(
-            z2[:].rearrange("p (c i t) -> p c t i", i=4, t=PACK),
-            larger[:].rearrange("p t (c i) -> p c t i", i=4),
-            gs_sb[:].unsqueeze(1).unsqueeze(3).to_broadcast([P, S // 4, PACK, 4]),
-            ALU.mult,
-        )
-        z2_codes = held("z2_codes", [P, S], U32)
+        def gain_y(t):
+            nc.gpsimd.tensor_scalar(yg[:, t, :], y[t][:, :S], gn_sb[:, t : t + 1], 0.0, ALU.mult, ALU.add)
+
+        z2 = ring.tile([P, PACK * S], BF16, name="z2", tag="z2", bufs=1, align_bytes=64)
+        z2_codes = ring.tile([P, S], U32, name="z2_codes", tag="z2_codes", bufs=1, align_bytes=64)
         z2_scales = held("z2_scales", [P, S], U8)
-        nc.vector.quantize_mx(out=z2_codes[:].bitcast(FP8X4), scales=z2_scales[:], in_=z2[:])
         b_ps = []
-        for t in range(PACK):
-            bank = psum.tile([P, S], F32, name="b_ps", tag="bank%d" % t)
-            nc.tensor.matmul_mx(
-                out=bank[:],
-                lhsT=xc_words[:, P * t : P * (t + 1)].bitcast(FP8X4),
-                lhsT_scale=xc_scales[:, P * t : P * (t + 1)],
-                rhs=z2_codes[:].bitcast(FP8X4),
-                rhs_scale=z2_scales[:],
-                start=True,
-                stop=True,
+
+        def scores():
+            nc.vector.tensor_copy(
+                z2[:].rearrange("p (c i t) -> p c t i", i=4, t=PACK),
+                weighted[:].rearrange("p t (c i) -> p c t i", i=4),
             )
-            b_ps.append(bank)
-        b = [held("b%d" % t, [P, S], F32) for t in range(PACK)]
+            nc.vector.quantize_mx(out=z2_codes[:].bitcast(FP8X4), scales=z2_scales[:], in_=z2[:])
+            for t in range(PACK):
+                bank = psum.tile([P, S], F32, name="b_ps", tag="bank%d" % t)
+                nc.tensor.matmul_mx(
+                    out=bank[:],
+                    lhsT=xc_words[:, P * t : P * (t + 1)].bitcast(FP8X4),
+                    lhsT_scale=xc_scales[:, P * t : P * (t + 1)],
+                    rhs=z2_codes[:].bitcast(FP8X4),
+                    rhs_scale=z2_scales[:],
+                    start=True,
+                    stop=True,
+                )
+                b_ps.append(bank)
 
-        sums3 = member_sums(3)
-        finish_z(2, sums2)
-        for t in (2, 3, 0, 1):
-            nc.scalar.copy(b[t][:], b_ps[t][:])
-        w2w, w2s = deal_weight("w2", w2w_raw, w2s_raw)
-        finish_z(3, sums3)
-        a_ps = {t: weight_product("bank%d" % (4 + (t + 2) % 4), w2w, w2s, z_codes, z_scales, t) for t in (2, 3, 0, 1)}
+        a_ps = {}
 
-        a = [held("a%d" % t, [P, S], F32) for t in range(PACK)]
+        def second_layer(first, width):
+            for t in TAIL_ORDER:
+                a_ps[t] = weight_product("bank%d" % t, w2w, w2s, z_codes, z_scales, t, slice(first, first + width), a_ps.get(t))
+
         gap = [held("gap%d" % t, [P, S], F32) for t in range(PACK)]
-        for t in (2, 0, 3, 1):
-            other = ring.tile([P, S], F32, name="other", tag="other", bufs=4)
-            for h in range(2):
-                gather("vector" if t >= 2 else "scalar", other[:, HALF * h : HALF * (h + 1)], b[t][:], entries(n4_sb, HALF * h, HALF))
-            nc.vector.tensor_tensor(gap[t][:], other[:], b_ps[t][:], ALU.subtract)
+
+        def score_out(t):
+            leave_psum(t in B_VECTOR, b[t][:, :S], b_ps[t][:])
+
+        def gate(t):
+            nc.scalar.activation(root_then_gate[:, t, :], gap[t][:], ACT.Sigmoid, scale=0.0625)
+
+        def score_gap(t, other):
+            other = fetch_row(t in N4_VECTOR, b[t], n4_sb, other)
+            nc.gpsimd.tensor_tensor(gap[t][:], other[:], b[t][:, :S], ALU.subtract)
+
+        for t in range(3):
+            member_sums(0, t, slot("early0%d" % t)[0])
+        member_sums(1, 0, slot("early10")[0])
+        for t in range(2):
+            scale_y(t)
+        for t in range(2):
+            larger_of_pair(t)
+        member_sums(1, 1, slot("pair1")[0])
+        member_sums(1, 2, slot("pair0")[0])
+        for t in range(2, 4):
+            scale_y(t)
+        for t in range(2, 4):
+            larger_of_pair(t)
+        member_sums(2, 0, slot("pair3")[0])
+        member_sums(0, 3, slot("early03")[0])
+        scores()
+        member_sums(1, 3, slot("weighted")[0])
+        after_z2 = slot("z2", 2)
+        member_sums(2, 1, after_z2[0])
+        member_sums(3, 0, after_z2[1])
+        for t in range(PACK):
+            gain_y(t)
+        w2w, w2s = deal_weight("w2", w2w_raw, w2s_raw, nc.gpsimd)
+        roots(0)
+        for t in TAIL_ORDER:
+            score_out(t)
+        roots(1)
+        score_gap(0, slot("early00")[0])
+        score_gap(1, slot("early01")[0])
+        member_sums(2, 3, slot("z2_codes")[0])
+        member_sums(2, 2, xc_next())
+        score_gap(2, slot("early02")[0])
+        member_sums(3, 3, slot("z2_codes")[0])
+        member_sums(3, 1, slot("early00")[0])
+        roots(2)
+        score_gap(3, xc_next())
+        member_sums(3, 2, slot("early01")[0])
+        roots(3)
+        finish_z(0, "early00")
+        finish_z(1, "early01")
+        second_layer(0, 2 * P)
+        finish_z(2, "early02")
+        second_layer(2 * P, P)
+        finish_z(3, "z2_codes")
+        second_layer(3 * P, P)
+        for t in TAIL_ORDER:
+            gate(t)
 
         result = held("result", [P, PACK, S], F32)
         out_codes = held("out_codes", [P, S], U32)
         out_scales = held("out_scales", [P, S], U8)
         out_rows = out_0.rearrange("(p t) c -> p t c", t=PACK)
         out_words = out_1[0].rearrange("p c r -> p (c r)").bitcast(I32)
-        for h in range(2):
-            cols = slice(HALF * h, HALF * (h + 1))
-            for t in (2, 3, 0, 1):
-                if h == 0:
-                    nc.scalar.activation(root_then_gate[:, t, :], gap[t][:], ACT.Sigmoid, scale=0.0625)
-                    nc.scalar.copy(a[t][:], a_ps[t][:])
-                other = ring.tile([P, HALF], F32, name="far", tag="far", bufs=8)
-                gather("scalar", other[:], a[t][:], entries(n3_sb, HALF * h, HALF))
-                step = ring.tile([P, HALF], F32, name="step", tag="step", bufs=2)
+        for first, width in CHUNKS:
+            cols = slice(first, first + width)
+            for t in TAIL_ORDER:
+                if first == 0:
+                    leave_psum(t in A_VECTOR, a[t][:], a_ps[t][:])
+                other = ring.tile([P, width], F32, name="far", tag="far", bufs=8)
+                gather((first, t) in N3_VECTOR, other[:], a[t][:], entries(n3_sb, first, width))
+                step = ring.tile([P, width], F32, name="step", tag="step", bufs=4)
                 nc.vector.tensor_tensor(step[:], other[:], a_ps[t][:, cols], ALU.subtract)
-                pull = ring.tile([P, HALF], F32, name="pull", tag="pull", bufs=2)
-                nc.vector.tensor_tensor(pull[:], step[:], root_then_gate[:, t, cols], ALU.mult)
+                pull = ring.tile([P, width], F32, name="pull", tag="pull", bufs=4)
+                (nc.gpsimd if first + width < S or t < 2 else nc.vector).tensor_tensor(pull[:], step[:], root_then_gate[:, t, cols], ALU.mult)
                 nc.vector.tensor_tensor(result[:, t, cols], pull[:], a_ps[t][:, cols], ALU.add)
             nc.sync.dma_start(out_rows[:, :, cols], result[:, :, cols])
-            rounded = ring.tile([P, PACK * HALF], BF16, name="rounded", tag="rounded", bufs=2, align_bytes=64)
-            nc.vector.tensor_copy(
+            rounded = ring.tile([P, PACK * width], BF16, name="rounded", tag="rounded", bufs=2, align_bytes=64)
+            (nc.scalar.copy if first in (0,) else nc.vector.tensor_copy)(
                 rounded[:].rearrange("p (c i t) -> p c t i", i=4, t=PACK),
                 result[:, :, cols].rearrange("p t (c i) -> p c t i", i=4),
             )

@@ -23,11 +23,11 @@ MEMBERS = 4
 BLOCKS = S // P
 N1_VECTOR = [(jb, t) for jb in range(4) for t in (0, 1, 2) if (jb, t) != (2, 2)]
 N2_VECTOR = ()
-N4_VECTOR = (0, 1, 2)
+N4_VECTOR = (0, 1)
 Y_VECTOR = ()
 B_VECTOR = ()
-A_VECTOR = (0,)
-N3_VECTOR = ((0, 0), (0, 2))
+A_VECTOR = (0, 1)
+N3_VECTOR = ()
 CHUNKS = ((0, 256), (256, 256))
 TAIL_ORDER = (0, 1, 2, 3)
 
@@ -125,15 +125,14 @@ def tile_picked_fkcdpullbgvarbig_none_po_kernel(
         nc.vector.tensor_copy(xq_words[:], xw[:].bitcast(U32).indirect(offs_sb[:]))
         w1w, w1s = deal_weight("w1", w1w_raw, w1s_raw, nc.vector)
 
-        def weight_product(tag, words, scales, codes, code_scales, t, cols=slice(0, S), bank=None):
-            if bank is None:
-                bank = psum.tile([P, S], F32, name=tag, tag=tag)
+        def weight_product(tag, words, scales, codes, code_scales, t):
+            bank = psum.tile([P, S], F32, name=tag, tag=tag)
             nc.tensor.matmul_mx(
-                out=bank[:, cols],
+                out=bank[:],
                 lhsT=words[:, 2 * P * t : 2 * P * (t + 1)].bitcast(FP4X4),
                 lhsT_scale=scales[:, P * t : P * (t + 1)],
-                rhs=codes[:, cols].bitcast(FP8X4),
-                rhs_scale=code_scales[:, cols],
+                rhs=codes[:].bitcast(FP8X4),
+                rhs_scale=code_scales[:],
                 start=True,
                 stop=True,
             )
@@ -142,7 +141,11 @@ def tile_picked_fkcdpullbgvarbig_none_po_kernel(
         y_ps = []
         for t in range(PACK):
             y_ps.append(weight_product("bank%d" % t, w1w, w1s, xq_words, xq_scales, t))
-            nc.scalar.activation(ysq[t][:, :S], y_ps[t][:], ACT.Square)
+            if t < 2:
+                nc.scalar.activation(ysq[t][:, :S], y_ps[t][:], ACT.Square)
+            else:
+                nc.scalar.copy(y[t][:, :S], y_ps[t][:])
+                nc.gpsimd.tensor_tensor(ysq[t][:, :S], y[t][:, :S], y[t][:, :S], ALU.mult)
 
         xc_words = held("xc_words", [P, S], U32, tag="w1s_raw")
         xc_next = lambda: held("after_cand", [P, S], F32, tag="w1s_raw")[:]
@@ -179,6 +182,7 @@ def tile_picked_fkcdpullbgvarbig_none_po_kernel(
                     nc.tensor.matmul(sums[jb][:, t, :], member, ident[:], start=(m == 0), stop=(m == MEMBERS - 1), is_transpose=True)
 
         backs = {}
+        z = held("z", [P, PACK * S], BF16)
 
         def roots(jb):
             cols = slice(P * jb, P * (jb + 1))
@@ -191,14 +195,15 @@ def tile_picked_fkcdpullbgvarbig_none_po_kernel(
         def finish_z(jb, tag):
             cols = slice(P * jb, P * (jb + 1))
             back = backs[jb]
-            z = ring.tile([P, PACK * P], BF16, name="z", tag=tag, bufs=1, align_bytes=64)
             nc.vector.tensor_tensor(
-                z[:].rearrange("p (c i t) -> p c t i", i=4, t=PACK),
+                z[:, PACK * P * jb : PACK * P * (jb + 1)].rearrange("p (c i t) -> p c t i", i=4, t=PACK),
                 back[:].rearrange("p t (c i) -> p c t i", i=4),
                 yg[:, :, cols].rearrange("p t (c i) -> p c t i", i=4),
                 ALU.mult,
             )
-            nc.vector.quantize_mx(out=z_codes[:, cols].bitcast(FP8X4), scales=z_scales[:, cols], in_=z[:])
+            if jb in (2, 3):
+                done = slice(0 if jb == 2 else P * jb, P * (jb + 1))
+                nc.vector.quantize_mx(out=z_codes[:, done].bitcast(FP8X4), scales=z_scales[:, done], in_=z[:, PACK * done.start : PACK * done.stop])
 
         def fetch_row(on_vector, source, offsets_tile, other):
             for e in range(0, S, piece):
@@ -240,12 +245,6 @@ def tile_picked_fkcdpullbgvarbig_none_po_kernel(
                 )
                 b_ps.append(bank)
 
-        a_ps = {}
-
-        def second_layer(first, width):
-            for t in TAIL_ORDER:
-                a_ps[t] = weight_product("bank%d" % t, w2w, w2s, z_codes, z_scales, t, slice(first, first + width), a_ps.get(t))
-
         gap = [held("gap%d" % t, [P, S], F32) for t in range(PACK)]
 
         def score_out(t):
@@ -268,11 +267,11 @@ def tile_picked_fkcdpullbgvarbig_none_po_kernel(
         member_sums(1, 1, slot("pair1")[0])
         member_sums(1, 2, slot("pair0")[0])
         for t in range(2, 4):
-            scale_y(t)
-        for t in range(2, 4):
             larger_of_pair(t)
         member_sums(2, 0, slot("pair3")[0])
         member_sums(0, 3, slot("early03")[0])
+        member_sums(2, 2, slot("early22")[0])
+        member_sums(2, 3, slot("early23")[0])
         scores()
         member_sums(1, 3, slot("weighted")[0])
         after_z2 = slot("z2", 2)
@@ -280,29 +279,29 @@ def tile_picked_fkcdpullbgvarbig_none_po_kernel(
         member_sums(3, 0, after_z2[1])
         for t in range(PACK):
             gain_y(t)
-        w2w, w2s = deal_weight("w2", w2w_raw, w2s_raw, nc.gpsimd)
+        w2w = ring.tile([P, 2 * S], U8, name="w2w", tag="larger", bufs=1, align_bytes=64)
+        nc.gpsimd.tensor_copy(w2w[:].rearrange("p (t m b) -> p m t b", t=PACK, b=2), w2w_raw[:].rearrange("p (m t b) -> p m t b", t=PACK, b=2))
+        w2s = ring.tile([P, S], U8, name="w2s", tag="weighted", bufs=1, align_bytes=64)
+        nc.gpsimd.tensor_copy(w2s[:].rearrange("p (t m) -> p m t", t=PACK), w2s_raw[:].rearrange("p (m t) -> p m t", t=PACK))
         roots(0)
         for t in TAIL_ORDER:
             score_out(t)
         roots(1)
         score_gap(0, slot("early00")[0])
         score_gap(1, slot("early01")[0])
-        member_sums(2, 3, slot("z2_codes")[0])
-        member_sums(2, 2, xc_next())
-        score_gap(2, slot("early02")[0])
-        member_sums(3, 3, slot("z2_codes")[0])
-        member_sums(3, 1, slot("early00")[0])
+        after_scores = slot("z2_codes", 3)
+        member_sums(3, 1, after_scores[2])
+        member_sums(3, 2, after_scores[0])
+        member_sums(3, 3, after_scores[1])
         roots(2)
-        score_gap(3, xc_next())
-        member_sums(3, 2, slot("early01")[0])
+        score_gap(2, slot("early02")[0])
+        score_gap(3, slot("early03")[0])
         roots(3)
         finish_z(0, "early00")
         finish_z(1, "early01")
-        second_layer(0, 2 * P)
         finish_z(2, "early02")
-        second_layer(2 * P, P)
         finish_z(3, "z2_codes")
-        second_layer(3 * P, P)
+        a_ps = {t: weight_product("bank%d" % (4 + TAIL_ORDER.index(t)), w2w, w2s, z_codes, z_scales, t) for t in TAIL_ORDER}
         for t in TAIL_ORDER:
             gate(t)
 
@@ -311,26 +310,29 @@ def tile_picked_fkcdpullbgvarbig_none_po_kernel(
         out_scales = held("out_scales", [P, S], U8)
         out_rows = out_0.rearrange("(p t) c -> p t c", t=PACK)
         out_words = out_1[0].rearrange("p c r -> p (c r)").bitcast(I32)
+        stay = held("stay", [P, PACK, S], F32)
+        for t in TAIL_ORDER:
+            leave_psum(t in A_VECTOR, a[t][:], a_ps[t][:])
+            nc.vector.scalar_tensor_tensor(stay[:, t, :], root_then_gate[:, t, :], -1.0, a_ps[t][:], ALU.add, ALU.mult)
         for first, width in CHUNKS:
             cols = slice(first, first + width)
             for t in TAIL_ORDER:
-                if first == 0:
-                    leave_psum(t in A_VECTOR, a[t][:], a_ps[t][:])
-                other = ring.tile([P, width], F32, name="far", tag="far", bufs=8)
+                other = held("far%d_%d" % (first, t), [P, width], F32)
                 gather((first, t) in N3_VECTOR, other[:], a[t][:], entries(n3_sb, first, width))
-                step = ring.tile([P, width], F32, name="step", tag="step", bufs=4)
-                nc.vector.tensor_tensor(step[:], other[:], a_ps[t][:, cols], ALU.subtract)
-                pull = ring.tile([P, width], F32, name="pull", tag="pull", bufs=4)
-                (nc.gpsimd if first + width < S or t < 2 else nc.vector).tensor_tensor(pull[:], step[:], root_then_gate[:, t, cols], ALU.mult)
-                nc.vector.tensor_tensor(result[:, t, cols], pull[:], a_ps[t][:, cols], ALU.add)
-            nc.sync.dma_start(out_rows[:, :, cols], result[:, :, cols])
+                pull = held("pull%d_%d" % (first, t), [P, width], F32)
+                nc.vector.tensor_tensor(pull[:], other[:], root_then_gate[:, t, cols], ALU.mult)
+                nc.vector.tensor_tensor(result[:, t, cols], pull[:], stay[:, t, cols], ALU.subtract)
+                if first > 0:
+                    nc.sync.dma_start(out_rows[:, t, cols], result[:, t, cols])
+            if first == 0:
+                nc.sync.dma_start(out_rows[:, :, cols], result[:, :, cols])
             rounded = ring.tile([P, PACK * width], BF16, name="rounded", tag="rounded", bufs=2, align_bytes=64)
             (nc.scalar.copy if first in (0,) else nc.vector.tensor_copy)(
                 rounded[:].rearrange("p (c i t) -> p c t i", i=4, t=PACK),
                 result[:, :, cols].rearrange("p t (c i) -> p c t i", i=4),
             )
             nc.vector.quantize_mx(out=out_codes[:, cols].bitcast(FP8X4), scales=out_scales[:, cols], in_=rounded[:])
-            nc.sync.dma_start(out_words[:, cols], out_codes[:, cols].bitcast(I32))
+            (nc.scalar if first else nc.sync).dma_start(out_words[:, cols], out_codes[:, cols].bitcast(I32))
         for q in range(4):
             queue = nc.scalar if q % 2 else nc.sync
             queue.dma_start(out_2[0, 4 * q : 4 * q + 4, :].bitcast(I32), out_scales[32 * q : 32 * q + 4, :].bitcast(I32))

@@ -26,7 +26,7 @@ N2_VECTOR = ()
 N4_VECTOR = (0, 1)
 Y_VECTOR = ()
 B_VECTOR = ()
-A_VECTOR = (0, 1)
+A_VECTOR = (0, 1, 2)
 N3_VECTOR = ()
 CHUNKS = ((0, 256), (256, 256))
 TAIL_ORDER = (0, 1, 2, 3)
@@ -58,9 +58,9 @@ def tile_picked_fkcdpullbgvarbig_none_po_kernel(
         def load_scale_quadrants(queue, name, src):
             width = src.shape[2]
             plane = held(name, [P, width], U8)
+            nc.gpsimd.memset(plane[:].bitcast(I32), 0)
             for q in range(4):
-                rows = src[0, 4 * q : 4 * q + 4, :].bitcast(I32)
-                queue.dma_start(plane[32 * q : 32 * (q + 1), :].bitcast(I32), rows.unsqueeze(0).to_broadcast([8, 4, width // 4]))
+                queue.dma_start(plane[32 * q : 32 * q + 4, :].bitcast(I32), src[0, 4 * q : 4 * q + 4, :].bitcast(I32))
             return plane
 
         def deal_weight(name, words, scales, byte_engine):
@@ -253,9 +253,13 @@ def tile_picked_fkcdpullbgvarbig_none_po_kernel(
         def gate(t):
             nc.scalar.activation(root_then_gate[:, t, :], gap[t][:], ACT.Sigmoid, scale=0.0625)
 
+        fetched_scores = {}
+
         def score_gap(t, other):
             other = fetch_row(t in N4_VECTOR, b[t], n4_sb, other)
-            nc.gpsimd.tensor_tensor(gap[t][:], other[:], b[t][:, :S], ALU.subtract)
+            fetched_scores[t] = other
+            if t < 3:
+                nc.gpsimd.tensor_tensor(gap[t][:], other[:], b[t][:, :S], ALU.subtract)
 
         for t in range(3):
             member_sums(0, t, slot("early0%d" % t)[0])
@@ -279,10 +283,10 @@ def tile_picked_fkcdpullbgvarbig_none_po_kernel(
         member_sums(3, 0, after_z2[1])
         for t in range(PACK):
             gain_y(t)
-        w2w = ring.tile([P, 2 * S], U8, name="w2w", tag="larger", bufs=1, align_bytes=64)
-        nc.gpsimd.tensor_copy(w2w[:].rearrange("p (t m b) -> p m t b", t=PACK, b=2), w2w_raw[:].rearrange("p (m t b) -> p m t b", t=PACK, b=2))
-        w2s = ring.tile([P, S], U8, name="w2s", tag="weighted", bufs=1, align_bytes=64)
-        nc.gpsimd.tensor_copy(w2s[:].rearrange("p (t m) -> p m t", t=PACK), w2s_raw[:].rearrange("p (m t) -> p m t", t=PACK))
+        w2w = held("w2w", [P, 2 * S], U8, tag="z2_scales")
+        nc.gpsimd.tensor_copy(w2w[:].rearrange("p (t m b) -> p t m b", t=PACK, b=2), w2w_raw[:].rearrange("p (m t b) -> p t m b", t=PACK, b=2))
+        w2s = held("w2s", [P, S], U8, tag="xc_scales")
+        nc.gpsimd.tensor_copy(w2s[:].rearrange("p (t m) -> p t m", t=PACK), w2s_raw[:].rearrange("p (m t) -> p t m", t=PACK))
         roots(0)
         for t in TAIL_ORDER:
             score_out(t)
@@ -295,12 +299,13 @@ def tile_picked_fkcdpullbgvarbig_none_po_kernel(
         member_sums(3, 3, after_scores[1])
         roots(2)
         score_gap(2, slot("early02")[0])
-        score_gap(3, slot("early03")[0])
         roots(3)
+        score_gap(3, slot("early03")[0])
         finish_z(0, "early00")
         finish_z(1, "early01")
         finish_z(2, "early02")
         finish_z(3, "z2_codes")
+        nc.vector.tensor_tensor(gap[3][:], fetched_scores[3], b_ps[3][:], ALU.subtract)
         a_ps = {t: weight_product("bank%d" % (4 + TAIL_ORDER.index(t)), w2w, w2s, z_codes, z_scales, t) for t in TAIL_ORDER}
         for t in TAIL_ORDER:
             gate(t)

@@ -105,6 +105,8 @@ def tile_picked_fkcdpullbgvarbig_none_po_kernel(
         n3_sb = load_list("n3_sb", n3)
         ident = held("ident", [P, P], F32)
         make_identity(nc, ident[:])
+        warm = held("warm", [P, 1], F32)
+        nc.scalar.activation(warm[:], ident[:, 0:1], ACT.Abs_reciprocal_sqrt, bias=0.5)
         ysq = [window("ysq%d" % t, 1024 if any((jb, t) in N1_VECTOR for jb in range(BLOCKS)) else 544) for t in range(PACK)]
         gn_sb = held("gn_sb", [P, PACK], F32)
         nc.gpsimd.dma_start(gn_sb[:], gn.rearrange("(p t) o -> p (t o)", t=PACK))

from contextlib import ExitStack

import concourse.mybir as mybir
from concourse.masks import make_identity

K, T, S, W = 512, 2048, 512, 2048
FLOPS = 3 * 2 * 512 * 512 * 512

F32 = mybir.dt.float32
BF16 = mybir.dt.bfloat16
I32 = mybir.dt.int32
U32 = mybir.dt.uint32
U16 = mybir.dt.uint16
U8 = mybir.dt.uint8
FP8X4 = mybir.dt.float8_e4m3fn_x4
FP4X4 = mybir.dt.float4_e2m1fn_x4
ACT = mybir.ActivationFunctionType
ALU = mybir.AluOpType

P = 128
PACK = 4
MEMBERS = 4
BLOCKS = S // P
N1_VECTOR = [(jb, t) for jb in range(4) for t in (0, 1, 2) if (jb, t) != (2, 2)]
N2_VECTOR = ()
N4_VECTOR = (0, 1)
Y_VECTOR = ()
B_VECTOR = ()
A_VECTOR = (0, 1, 2)
N3_VECTOR = ()
CHUNKS = ((0, 256), (256, 256))
TAIL_ORDER = (0, 1, 2, 3)


def tile_picked_fkcdpullbgvarbig_none_po_kernel(
    tc, x_words, x_scales, w1_words, w1_scales, gn, w2_words, w2_scales, gs, offs, n1, n2, cand, n3, n4, out_0, out_1, out_2
):
    nc = tc.nc
    with ExitStack() as ctx:
        keep = ctx.enter_context(tc.tile_pool(name="keep", bufs=1))
        ring = ctx.enter_context(tc.tile_pool(name="ring", bufs=1))
        psum = ctx.enter_context(tc.psum_pool(name="psum", bufs=1))

        def held(name, shape, dtype, tag=""):
            return keep.tile(shape, dtype, name=name, tag=tag or name, align_bytes=64)

        def window(name, width):
            tile = held(name, [P, width], F32)
            if width > S:
                nc.gpsimd.memset(tile[:, S:], 0.0)
            return tile

        def load_list(name, src):
            tile = keep.tile(list(src.shape), U16, name=name)
            nc.sync.dma_start(tile[:], src)
            return tile

        def load_scale_quadrants(queue, name, src):
            width = src.shape[2]
            plane = held(name, [P, width], U8)
            nc.gpsimd.memset(plane[:].bitcast(I32), 0)
            for q in range(4):
                queue.dma_start(plane[32 * q : 32 * q + 4, :].bitcast(I32), src[0, 4 * q : 4 * q + 4, :].bitcast(I32))
            return plane

        def deal_weight(name, words, scales, byte_engine):
            dealt_words = held(name + "_words", [P, 2 * S], U8)
            nc.scalar.copy(
                dealt_words[:].bitcast(U16).rearrange("p (t m) -> p t m", t=PACK),
                words[:].bitcast(U16).rearrange("p (m t) -> p t m", t=PACK),
            )
            dealt_scales = held(name + "_scales", [P, S], U8)
            byte_engine.tensor_copy(
                dealt_scales[:].rearrange("p (t m) -> p m t", t=PACK),
                scales[:].rearrange("p (m t) -> p m t", t=PACK),
            )
            return dealt_words, dealt_scales

        def entries(tile, start, count):
            return tile[:, start // 16 : (start + count) // 16]

        def gather(on_vector, out, source, offsets):
            if on_vector:
                nc.vector.tensor_copy(out, source.indirect(offsets))
            else:
                nc.scalar.activation(out, source.indirect(offsets), ACT.Copy)

        def leave_psum(on_vector, out, bank):
            if on_vector:
                nc.vector.tensor_copy(out, bank)
            else:
                nc.scalar.copy(out, bank)

        offs_sb = load_list("offs_sb", offs)
        cand_sb = load_list("cand_sb", cand)
        xs = load_scale_quadrants(nc.sync, "xs", x_scales)
        w1w_raw = held("w1w_raw", [P, 2 * S], U8)
        nc.sync.dma_start(w1w_raw[:].bitcast(I32), w1_words[0].bitcast(I32))
        xw = held("xw", [P, T], I32)
        nc.sync.dma_start(xw[:], x_words[0].rearrange("p c r -> p (c r)").bitcast(I32))
        w1s_raw = load_scale_quadrants(nc.sync, "w1s_raw", w1_scales)
        n1_sb = load_list("n1_sb", n1)
        n2_sb = load_list("n2_sb", n2)
        n4_sb = load_list("n4_sb", n4)
        n3_sb = load_list("n3_sb", n3)
        ident = held("ident", [P, P], F32)
        make_identity(nc, ident[:])
        warm = held("warm", [P, 1], F32)
        nc.scalar.activation(warm[:], ident[:, 0:1], ACT.Abs_reciprocal_sqrt, bias=0.5)
        ysq = [window("ysq%d" % t, 1024 if any((jb, t) in N1_VECTOR for jb in range(BLOCKS)) else 544) for t in range(PACK)]
        gn_sb = held("gn_sb", [P, PACK], F32)
        nc.gpsimd.dma_start(gn_sb[:], gn.rearrange("(p t) o -> p (t o)", t=PACK))
        gs_sb = held("gs_sb", [P, PACK], F32)
        nc.gpsimd.dma_start(gs_sb[:], gs.rearrange("(p t) o -> p (t o)", t=PACK))
        y = [window("y%d" % t, 704 if t in N2_VECTOR else 544) for t in range(PACK)]
        b = [window("b%d" % t, 704 if t in N4_VECTOR else 544) for t in range(PACK)]
        a = [held("a%d" % t, [P, S], F32) for t in range(PACK)]
        w2w_raw = held("w2w_raw", [P, 2 * S], U8)
        nc.sync.dma_start(w2w_raw[:].bitcast(I32), w2_words[0].bitcast(I32))
        w2s_raw = load_scale_quadrants(nc.sync, "w2s_raw", w2_scales)

        xq_scales = held("xq_scales", [P, S], U8)
        nc.vector.tensor_copy(xq_scales[:], xs[:].indirect(offs_sb[:]))
        xc_scales = held("xc_scales", [P, S], U8)
        nc.vector.tensor_copy(xc_scales[:].rearrange("p (t m) -> p m t", t=PACK), xs[:].indirect(cand_sb[:]))
        xq_words = held("xq_words", [P, S], U32)
        nc.vector.tensor_copy(xq_words[:], xw[:].bitcast(U32).indirect(offs_sb[:]))
        w1w, w1s = deal_weight("w1", w1w_raw, w1s_raw, nc.vector)

        def weight_product(tag, words, scales, codes, code_scales, t):
            bank = psum.tile([P, S], F32, name=tag, tag=tag)
            nc.tensor.matmul_mx(
                out=bank[:],
                lhsT=words[:, 2 * P * t : 2 * P * (t + 1)].bitcast(FP4X4),
                lhsT_scale=scales[:, P * t : P * (t + 1)],
                rhs=codes[:].bitcast(FP8X4),
                rhs_scale=code_scales[:],
                start=True,
                stop=True,
            )
            return bank

        y_ps = []
        for t in range(PACK):
            y_ps.append(weight_product("bank%d" % t, w1w, w1s, xq_words, xq_scales, t))
            if t < 2:
                nc.scalar.activation(ysq[t][:, :S], y_ps[t][:], ACT.Square)
            else:
                nc.scalar.copy(y[t][:, :S], y_ps[t][:])
                nc.gpsimd.tensor_tensor(ysq[t][:, :S], y[t][:, :S], y[t][:, :S], ALU.mult)

        xc_words = held("xc_words", [P, S], U32, tag="w1s_raw")
        xc_next = lambda: held("after_cand", [P, S], F32, tag="w1s_raw")[:]
        nc.vector.tensor_copy(xc_words[:].rearrange("p (t m) -> p m t", t=PACK), xw[:].bitcast(U32).indirect(cand_sb[:]))

        yg = held("yg", [P, PACK, S], F32)
        root_then_gate = held("root_then_gate", [P, PACK, S], F32)
        z_codes = held("z_codes", [P, S], U32)
        z_scales = held("z_scales", [P, S], U8)
        larger = ring.tile([P, PACK, S], F32, name="larger", tag="larger", bufs=1, align_bytes=64)
        weighted = ring.tile([P, PACK, S], BF16, name="weighted", tag="weighted", bufs=1, align_bytes=64)
        piece = 512

        sums = {}

        def slot(tag, count=1):
            tile = ring.tile([P, count, S], F32, name=tag, tag=tag, bufs=1, align_bytes=64)
            return [tile[:, k, :] for k in range(count)]

        def member_sums(jb, t, fetched):
            if jb not in sums:
                sums[jb] = psum.tile([P, PACK, P], F32, name="sums", tag="bank%d" % (4 + jb))
            if True:
                on_vector = (jb, t) in N1_VECTOR
                for e in range(0, MEMBERS * P, piece):
                    offsets = entries(n1_sb, MEMBERS * P * jb + e, piece)
                    if on_vector:
                        planes = fetched.rearrange("p (m j) -> p j m", m=MEMBERS)
                        gather(True, planes[:, e // MEMBERS : (e + piece) // MEMBERS, :], ysq[t][:], offsets)
                    else:
                        gather(False, fetched[:, e : e + piece], ysq[t][:], offsets)
                for m in range(MEMBERS):
                    member = fetched[:, P * m : P * (m + 1)] if on_vector else fetched[:, m : MEMBERS * P : MEMBERS]
                    nc.tensor.matmul(sums[jb][:, t, :], member, ident[:], start=(m == 0), stop=(m == MEMBERS - 1), is_transpose=True)

        backs = {}
        z = held("z", [P, PACK * S], BF16)

        def roots(jb):
            cols = slice(P * jb, P * (jb + 1))
            nc.scalar.activation(root_then_gate[:, :, cols], sums[jb][:], ACT.Abs_reciprocal_sqrt, bias=0.5)
            back = psum.tile([P, PACK, P], F32, name="back", tag="bank%d" % (4 + jb))
            for t in range(PACK):
                nc.tensor.transpose(back[:, t, :], root_then_gate[:, t, cols], ident[:])
            backs[jb] = back

        def finish_z(jb, tag):
            cols = slice(P * jb, P * (jb + 1))
            back = backs[jb]
            nc.vector.tensor_tensor(
                z[:, PACK * P * jb : PACK * P * (jb + 1)].rearrange("p (c i t) -> p c t i", i=4, t=PACK),
                back[:].rearrange("p t (c i) -> p c t i", i=4),
                yg[:, :, cols].rearrange("p t (c i) -> p c t i", i=4),
                ALU.mult,
            )
            if jb in (2, 3):
                done = slice(0 if jb == 2 else P * jb, P * (jb + 1))
                nc.vector.quantize_mx(out=z_codes[:, done].bitcast(FP8X4), scales=z_scales[:, done], in_=z[:, PACK * done.start : PACK * done.stop])

        def fetch_row(on_vector, source, offsets_tile, other):
            for e in range(0, S, piece):
                gather(on_vector, other[:, e : e + piece], source[:], entries(offsets_tile, e, piece))
            return other

        def larger_of_pair(t):
            other = fetch_row(t in N2_VECTOR, y[t], n2_sb, slot("pair%d" % t)[0])
            nc.vector.tensor_tensor(larger[:, t, :], other[:], y_ps[t][:], ALU.max)
            nc.gpsimd.tensor_scalar(weighted[:, t, :], larger[:, t, :], gs_sb[:, t : t + 1], 0.0, ALU.mult, ALU.add)

        def scale_y(t):
            leave_psum(t in Y_VECTOR, y[t][:, :S], y_ps[t][:])

        def gain_y(t):
            nc.gpsimd.tensor_scalar(yg[:, t, :], y[t][:, :S], gn_sb[:, t : t + 1], 0.0, ALU.mult, ALU.add)

        z2 = ring.tile([P, PACK * S], BF16, name="z2", tag="z2", bufs=1, align_bytes=64)
        z2_codes = ring.tile([P, S], U32, name="z2_codes", tag="z2_codes", bufs=1, align_bytes=64)
        z2_scales = held("z2_scales", [P, S], U8)
        b_ps = []

        def scores():
            nc.vector.tensor_copy(
                z2[:].rearrange("p (c i t) -> p c t i", i=4, t=PACK),
                weighted[:].rearrange("p t (c i) -> p c t i", i=4),
            )
            nc.vector.quantize_mx(out=z2_codes[:].bitcast(FP8X4), scales=z2_scales[:], in_=z2[:])
            for t in range(PACK):
                bank = psum.tile([P, S], F32, name="b_ps", tag="bank%d" % t)
                nc.tensor.matmul_mx(
                    out=bank[:],
                    lhsT=xc_words[:, P * t : P * (t + 1)].bitcast(FP8X4),
                    lhsT_scale=xc_scales[:, P * t : P * (t + 1)],
                    rhs=z2_codes[:].bitcast(FP8X4),
                    rhs_scale=z2_scales[:],
                    start=True,
                    stop=True,
                )
                b_ps.append(bank)

        gap = [held("gap%d" % t, [P, S], F32) for t in range(PACK)]

        def score_out(t):
            leave_psum(t in B_VECTOR, b[t][:, :S], b_ps[t][:])

        def gate(t):
            nc.scalar.activation(root_then_gate[:, t, :], gap[t][:], ACT.Sigmoid, scale=0.0625)

        fetched_scores = {}

        def score_gap(t, other):
            other = fetch_row(t in N4_VECTOR, b[t], n4_sb, other)
            fetched_scores[t] = other
            if t < 3:
                nc.gpsimd.tensor_tensor(gap[t][:], other[:], b[t][:, :S], ALU.subtract)

        for t in range(3):
            member_sums(0, t, slot("early0%d" % t)[0])
        member_sums(1, 0, slot("early10")[0])
        for t in range(2):
            scale_y(t)
        for t in range(2):
            larger_of_pair(t)
        member_sums(1, 1, slot("pair1")[0])
        member_sums(1, 2, slot("pair0")[0])
        for t in range(2, 4):
            larger_of_pair(t)
        member_sums(2, 0, slot("pair3")[0])
        member_sums(0, 3, slot("early03")[0])
        member_sums(2, 2, slot("early22")[0])
        member_sums(2, 3, slot("early23")[0])
        scores()
        member_sums(1, 3, slot("weighted")[0])
        after_z2 = slot("z2", 2)
        member_sums(2, 1, after_z2[0])
        member_sums(3, 0, after_z2[1])
        for t in range(PACK):
            gain_y(t)
        w2w = held("w2w", [P, 2 * S], U8, tag="z2_scales")
        nc.gpsimd.tensor_copy(w2w[:].rearrange("p (t m b) -> p t m b", t=PACK, b=2), w2w_raw[:].rearrange("p (m t b) -> p t m b", t=PACK, b=2))
        w2s = held("w2s", [P, S], U8, tag="xc_scales")
        nc.gpsimd.tensor_copy(w2s[:].rearrange("p (t m) -> p t m", t=PACK), w2s_raw[:].rearrange("p (m t) -> p t m", t=PACK))
        roots(0)
        for t in TAIL_ORDER:
            score_out(t)
        roots(1)
        score_gap(0, slot("early00")[0])
        score_gap(1, slot("early01")[0])
        after_scores = slot("z2_codes", 3)
        member_sums(3, 1, after_scores[2])
        member_sums(3, 2, after_scores[0])
        member_sums(3, 3, after_scores[1])
        roots(2)
        score_gap(2, slot("early02")[0])
        roots(3)
        score_gap(3, slot("early03")[0])
        finish_z(0, "early00")
        finish_z(1, "early01")
        finish_z(2, "early02")
        finish_z(3, "z2_codes")
        nc.vector.tensor_tensor(gap[3][:], fetched_scores[3], b_ps[3][:], ALU.subtract)
        a_ps = {t: weight_product("bank%d" % (4 + TAIL_ORDER.index(t)), w2w, w2s, z_codes, z_scales, t) for t in TAIL_ORDER}
        for t in TAIL_ORDER:
            gate(t)

        result = held("result", [P, PACK, S], F32)
        out_codes = held("out_codes", [P, S], U32)
        out_scales = held("out_scales", [P, S], U8)
        out_rows = out_0.rearrange("(p t) c -> p t c", t=PACK)
        out_words = out_1[0].rearrange("p c r -> p (c r)").bitcast(I32)
        stay = held("stay", [P, PACK, S], F32)
        for t in TAIL_ORDER:
            leave_psum(t in A_VECTOR, a[t][:], a_ps[t][:])
            nc.vector.scalar_tensor_tensor(stay[:, t, :], root_then_gate[:, t, :], -1.0, a_ps[t][:], ALU.add, ALU.mult)
        for first, width in CHUNKS:
            cols = slice(first, first + width)
            for t in TAIL_ORDER:
                other = held("far%d_%d" % (first, t), [P, width], F32)
                gather((first, t) in N3_VECTOR, other[:], a[t][:], entries(n3_sb, first, width))
                pull = held("pull%d_%d" % (first, t), [P, width], F32)
                nc.vector.tensor_tensor(pull[:], other[:], root_then_gate[:, t, cols], ALU.mult)
                nc.vector.tensor_tensor(result[:, t, cols], pull[:], stay[:, t, cols], ALU.subtract)
                if first > 0:
                    nc.sync.dma_start(out_rows[:, t, cols], result[:, t, cols])
            if first == 0:
                nc.sync.dma_start(out_rows[:, :, cols], result[:, :, cols])
            rounded = ring.tile([P, PACK * width], BF16, name="rounded", tag="rounded", bufs=2, align_bytes=64)
            (nc.scalar.copy if first in (0,) else nc.vector.tensor_copy)(
                rounded[:].rearrange("p (c i t) -> p c t i", i=4, t=PACK),
                result[:, :, cols].rearrange("p t (c i) -> p c t i", i=4),
            )
            nc.vector.quantize_mx(out=out_codes[:, cols].bitcast(FP8X4), scales=out_scales[:, cols], in_=rounded[:])
            (nc.scalar if first else nc.sync).dma_start(out_words[:, cols], out_codes[:, cols].bitcast(I32))
        for q in range(4):
            queue = nc.scalar if q % 2 else nc.sync
            queue.dma_start(out_2[0, 4 * q : 4 * q + 4, :].bitcast(I32), out_scales[32 * q : 32 * q + 4, :].bitcast(I32))
